import numpy as np, ml_dtypes
CORES = [12,28,44,60,3,19,35,51]
N = 8
TOK, K, FT = 512, 1, 1
ROUTE = [[[3],[2],[7],[7],[0],[6],[1],[0],[4],[5],[7],[2],[7],[6],[4],[7],[2],[0],[1],[7],[0],[0],[0],[6],[4],[4],[6],[7],[1],[5],[4],[3],[2],[4],[4],[6],[4],[4],[3],[7],[5],[6],[4],[0],[2],[6],[5],[1],[1],[3],[4],[4],[0],[2],[7],[4],[7],[3],[0],[4],[1],[4],[6],[3],[5],[7],[1],[4],[7],[4],[7],[7],[7],[6],[5],[7],[7],[2],[5],[6],[2],[7],[2],[7],[4],[3],[3],[4],[0],[3],[6],[4],[7],[4],[7],[6],[1],[3],[3],[3],[0],[5],[7],[1],[2],[2],[2],[1],[7],[3],[6],[3],[5],[7],[1],[5],[3],[7],[2],[1],[1],[2],[5],[4],[5],[6],[3],[5],[2],[4],[4],[0],[0],[0],[3],[7],[4],[2],[0],[1],[7],[0],[2],[6],[2],[0],[4],[4],[3],[2],[5],[7],[0],[3],[3],[0],[1],[2],[6],[5],[5],[2],[0],[6],[2],[6],[6],[7],[0],[0],[3],[4],[3],[7],[7],[6],[1],[2],[6],[6],[5],[0],[3],[0],[1],[2],[1],[0],[3],[2],[5],[2],[1],[5],[0],[6],[0],[4],[2],[5],[5],[1],[5],[6],[1],[5],[5],[4],[3],[0],[1],[7],[6],[7],[4],[6],[6],[6],[2],[0],[6],[7],[5],[5],[7],[1],[5],[5],[3],[6],[5],[0],[4],[1],[4],[4],[6],[6],[3],[4],[3],[0],[2],[6],[1],[1],[7],[0],[0],[0],[1],[1],[4],[2],[3],[4],[5],[1],[7],[2],[7],[7],[1],[7],[6],[5],[2],[5],[3],[2],[2],[0],[6],[2],[4],[1],[5],[7],[2],[5],[2],[7],[7],[2],[4],[4],[0],[6],[5],[1],[5],[1],[0],[7],[3],[0],[7],[2],[5],[0],[1],[7],[5],[7],[0],[2],[6],[3],[4],[2],[4],[1],[5],[5],[6],[3],[2],[3],[5],[5],[1],[3],[1],[7],[7],[4],[7],[4],[4],[5],[2],[2],[4],[6],[5],[0],[1],[4],[5],[1],[1],[3],[6],[4],[4],[5],[3],[6],[5],[2],[7],[5],[0],[4],[5],[5],[0],[0],[4],[2],[0],[6],[3],[5],[0],[5],[5],[5],[3],[5],[3],[4],[4],[2],[2],[0],[5],[3],[1],[0],[7],[3],[5],[2],[5],[3],[1],[5],[5],[2],[2],[1],[7],[2],[6],[2],[6],[4],[6],[1],[5],[2],[2],[7],[0],[7],[4],[6],[7],[1],[6],[4],[0],[3],[1],[5],[6],[5],[2],[3],[5],[2],[5],[4],[4],[4],[2],[5],[7],[2],[6],[4],[5],[5],[5],[4],[1],[4],[7],[6],[2],[7],[2],[7],[7],[7],[3],[1],[7],[5],[7],[2],[0],[1],[3],[3],[3],[0],[5],[0],[1],[2],[7],[3],[3],[6],[2],[4],[5],[7],[2],[1],[6],[6],[7],[7],[5],[2],[5],[2],[2],[7],[7],[1],[6],[6],[3],[1],[7],[5],[6],[1],[7],[2],[7],[6],[0],[6],[0],[7],[6],[1],[3],[2],[6],[1],[2],[1],[2],[4],[4],[1]],[[6],[4],[2],[5],[0],[7],[3],[5],[0],[2],[6],[0],[0],[5],[6],[0],[2],[1],[5],[4],[5],[1],[0],[7],[2],[4],[0],[7],[6],[2],[4],[6],[7],[4],[3],[0],[1],[1],[5],[5],[7],[4],[3],[4],[3],[4],[0],[0],[1],[7],[4],[1],[4],[6],[1],[6],[5],[6],[7],[1],[6],[6],[4],[7],[6],[0],[2],[6],[0],[2],[5],[2],[7],[1],[0],[2],[5],[5],[2],[1],[4],[1],[1],[1],[6],[4],[5],[4],[0],[5],[1],[2],[3],[6],[3],[3],[5],[3],[6],[7],[0],[5],[6],[4],[5],[1],[5],[3],[6],[4],[0],[7],[7],[3],[5],[7],[2],[3],[7],[2],[2],[4],[0],[4],[6],[3],[0],[6],[2],[0],[5],[6],[7],[6],[5],[5],[5],[0],[3],[4],[5],[6],[3],[4],[4],[0],[5],[4],[3],[4],[2],[2],[5],[2],[2],[0],[7],[7],[0],[2],[6],[3],[3],[2],[5],[7],[0],[2],[7],[1],[3],[6],[4],[3],[6],[5],[4],[6],[5],[0],[6],[7],[6],[1],[1],[3],[3],[5],[2],[5],[6],[2],[4],[5],[6],[5],[2],[7],[5],[3],[0],[5],[3],[4],[5],[6],[6],[4],[7],[6],[7],[2],[1],[5],[4],[3],[7],[3],[3],[7],[2],[7],[1],[0],[1],[2],[6],[0],[4],[2],[1],[0],[6],[2],[4],[4],[1],[0],[0],[4],[6],[6],[3],[1],[1],[3],[2],[2],[2],[0],[4],[4],[6],[5],[0],[6],[2],[5],[4],[3],[0],[7],[6],[2],[6],[0],[1],[0],[1],[3],[5],[5],[4],[7],[3],[3],[2],[0],[4],[0],[0],[2],[5],[1],[3],[1],[0],[1],[0],[2],[1],[4],[6],[0],[0],[2],[1],[4],[6],[5],[7],[5],[7],[4],[3],[5],[1],[4],[7],[1],[7],[1],[6],[3],[5],[3],[0],[3],[6],[7],[3],[3],[6],[0],[7],[0],[2],[2],[6],[0],[1],[7],[5],[6],[4],[4],[7],[7],[5],[6],[4],[2],[3],[1],[3],[0],[5],[2],[3],[6],[0],[7],[7],[7],[2],[4],[0],[3],[7],[7],[5],[5],[7],[3],[5],[4],[3],[0],[3],[0],[3],[6],[0],[6],[2],[1],[0],[6],[4],[5],[2],[3],[7],[4],[4],[6],[5],[7],[0],[7],[7],[5],[5],[2],[1],[3],[2],[1],[2],[5],[2],[1],[4],[7],[2],[6],[0],[2],[1],[0],[6],[0],[7],[5],[7],[0],[6],[3],[7],[3],[6],[1],[5],[1],[5],[7],[4],[4],[6],[2],[4],[7],[3],[1],[7],[6],[1],[3],[3],[1],[3],[2],[4],[5],[1],[7],[4],[6],[6],[1],[4],[0],[2],[3],[0],[4],[3],[7],[7],[0],[1],[5],[2],[6],[7],[1],[5],[4],[2],[7],[1],[6],[5],[3],[0],[5],[2],[7],[6],[7],[2],[5],[3],[6],[6],[3],[3],[6],[5],[1],[3],[6],[2],[5],[1],[1],[2],[2],[2],[5],[0],[3],[5],[6],[5],[7],[7],[5],[5],[7],[2],[4]],[[7],[6],[5],[7],[1],[4],[1],[3],[7],[4],[5],[5],[6],[4],[1],[4],[3],[3],[4],[5],[7],[2],[0],[2],[7],[7],[3],[3],[0],[6],[2],[7],[4],[1],[0],[7],[3],[3],[7],[6],[3],[1],[3],[3],[5],[3],[4],[5],[1],[0],[2],[1],[2],[5],[2],[7],[0],[7],[1],[3],[4],[0],[6],[6],[4],[0],[7],[4],[6],[7],[7],[3],[2],[7],[6],[5],[7],[0],[3],[7],[2],[1],[3],[0],[1],[7],[0],[7],[5],[1],[4],[5],[4],[6],[0],[0],[0],[6],[4],[4],[3],[3],[6],[4],[5],[1],[4],[5],[5],[6],[5],[4],[1],[2],[6],[4],[6],[5],[5],[1],[7],[3],[5],[2],[5],[2],[4],[2],[0],[7],[2],[1],[0],[5],[7],[7],[5],[1],[1],[2],[5],[2],[4],[1],[0],[3],[1],[7],[6],[2],[0],[3],[4],[4],[2],[3],[2],[4],[3],[6],[2],[1],[3],[5],[0],[0],[3],[3],[5],[4],[5],[0],[0],[7],[1],[2],[3],[6],[4],[1],[3],[4],[0],[0],[4],[6],[7],[3],[1],[7],[7],[4],[0],[2],[4],[4],[2],[2],[3],[5],[6],[3],[2],[5],[0],[6],[7],[5],[0],[6],[4],[5],[6],[5],[0],[3],[5],[4],[2],[7],[2],[2],[4],[0],[0],[2],[2],[2],[2],[5],[6],[2],[3],[3],[6],[3],[5],[7],[1],[7],[0],[2],[1],[0],[2],[6],[1],[1],[0],[1],[2],[6],[3],[7],[1],[1],[5],[7],[1],[0],[4],[0],[4],[4],[0],[4],[6],[2],[5],[3],[2],[6],[0],[6],[6],[3],[2],[0],[3],[7],[2],[7],[5],[5],[2],[7],[7],[3],[7],[4],[6],[6],[6],[1],[7],[2],[4],[3],[4],[5],[5],[0],[5],[3],[2],[2],[3],[3],[6],[0],[1],[4],[0],[0],[7],[1],[0],[6],[6],[7],[7],[5],[1],[2],[4],[4],[5],[4],[1],[0],[1],[3],[2],[3],[2],[3],[0],[1],[7],[6],[6],[6],[7],[4],[3],[1],[1],[4],[3],[0],[0],[5],[4],[5],[5],[6],[5],[1],[0],[3],[4],[5],[6],[2],[3],[1],[6],[5],[1],[7],[2],[3],[4],[0],[5],[6],[5],[7],[0],[4],[7],[5],[3],[2],[4],[4],[3],[4],[3],[0],[0],[6],[4],[6],[5],[0],[0],[5],[7],[5],[3],[5],[4],[3],[3],[2],[1],[4],[0],[7],[4],[1],[6],[7],[5],[4],[7],[0],[3],[6],[5],[7],[2],[7],[5],[0],[3],[5],[0],[6],[7],[2],[6],[4],[2],[2],[1],[6],[0],[5],[5],[2],[7],[3],[2],[4],[0],[4],[2],[4],[7],[6],[0],[6],[5],[1],[3],[4],[1],[1],[1],[4],[5],[7],[5],[3],[5],[6],[7],[3],[3],[0],[7],[7],[5],[4],[2],[4],[1],[1],[1],[3],[4],[4],[4],[4],[5],[3],[0],[6],[5],[3],[3],[2],[2],[3],[6],[4],[1],[5],[2],[7],[0],[6],[5],[6],[4],[4],[1],[5],[7],[0]],[[3],[3],[1],[5],[2],[4],[6],[1],[5],[6],[0],[6],[0],[3],[5],[6],[5],[5],[2],[5],[4],[6],[1],[4],[7],[3],[6],[2],[4],[2],[1],[2],[7],[0],[0],[4],[1],[7],[2],[7],[4],[7],[5],[7],[1],[1],[7],[4],[3],[6],[4],[0],[6],[4],[0],[4],[3],[5],[4],[0],[7],[0],[7],[0],[6],[6],[1],[1],[0],[4],[5],[4],[3],[6],[5],[5],[4],[6],[0],[7],[4],[0],[2],[4],[0],[4],[6],[3],[4],[4],[2],[2],[0],[3],[3],[1],[5],[4],[7],[6],[6],[4],[3],[0],[1],[7],[6],[5],[4],[1],[1],[7],[0],[0],[0],[7],[7],[5],[1],[4],[1],[3],[2],[6],[1],[7],[2],[0],[6],[4],[4],[5],[2],[4],[3],[6],[6],[0],[4],[5],[1],[3],[2],[0],[2],[1],[7],[5],[3],[5],[5],[5],[6],[2],[3],[7],[5],[6],[1],[2],[0],[5],[7],[1],[3],[5],[2],[2],[0],[2],[0],[3],[2],[1],[1],[2],[1],[0],[6],[2],[4],[4],[4],[3],[7],[3],[5],[3],[5],[2],[0],[5],[2],[4],[0],[6],[5],[4],[0],[3],[4],[4],[3],[5],[1],[0],[7],[3],[1],[3],[7],[7],[6],[6],[6],[6],[0],[2],[7],[3],[7],[6],[4],[5],[7],[6],[7],[2],[6],[4],[2],[4],[4],[4],[6],[1],[5],[7],[4],[2],[5],[0],[5],[0],[6],[5],[1],[3],[6],[4],[5],[6],[5],[6],[0],[7],[5],[4],[6],[4],[0],[1],[3],[3],[5],[2],[3],[4],[7],[2],[7],[1],[2],[6],[1],[3],[5],[0],[4],[0],[7],[3],[5],[6],[6],[6],[3],[1],[1],[3],[4],[6],[7],[7],[3],[7],[3],[4],[7],[2],[2],[2],[3],[2],[3],[1],[3],[2],[5],[3],[6],[4],[5],[2],[4],[5],[6],[7],[1],[7],[7],[6],[0],[2],[7],[7],[6],[3],[6],[3],[7],[2],[1],[4],[2],[6],[1],[1],[5],[1],[4],[7],[6],[2],[4],[3],[7],[7],[0],[4],[6],[0],[0],[1],[3],[0],[1],[7],[1],[0],[7],[6],[6],[2],[6],[2],[1],[2],[5],[2],[7],[4],[2],[2],[0],[7],[0],[0],[5],[3],[3],[4],[6],[5],[4],[5],[0],[7],[3],[0],[1],[6],[7],[7],[0],[0],[0],[5],[6],[7],[2],[0],[0],[2],[4],[4],[1],[6],[7],[2],[3],[7],[6],[4],[6],[6],[6],[3],[6],[3],[6],[4],[7],[5],[1],[2],[2],[4],[5],[5],[6],[7],[6],[2],[1],[3],[5],[6],[5],[2],[2],[4],[1],[1],[4],[6],[4],[5],[2],[6],[0],[1],[0],[7],[5],[1],[2],[3],[3],[7],[4],[7],[1],[5],[7],[5],[0],[7],[3],[4],[0],[3],[6],[4],[1],[1],[6],[6],[5],[6],[3],[4],[0],[6],[7],[6],[0],[2],[7],[4],[7],[5],[7],[4],[4],[7],[5],[1],[2],[0],[7],[2],[3],[3],[7],[0],[7],[2],[6],[6],[4],[4]],[[3],[0],[2],[6],[1],[0],[2],[0],[4],[3],[3],[3],[2],[0],[5],[5],[5],[0],[6],[4],[2],[4],[0],[0],[7],[0],[6],[0],[5],[5],[5],[6],[2],[5],[2],[1],[4],[6],[0],[2],[5],[5],[0],[5],[1],[6],[2],[1],[3],[0],[3],[2],[4],[4],[2],[7],[4],[2],[6],[6],[4],[6],[2],[4],[4],[5],[5],[5],[1],[5],[6],[6],[2],[4],[7],[2],[6],[2],[2],[1],[3],[4],[3],[4],[0],[7],[2],[0],[0],[6],[3],[7],[3],[5],[4],[5],[2],[3],[1],[3],[1],[3],[4],[2],[2],[3],[6],[7],[7],[5],[0],[0],[6],[2],[0],[3],[1],[6],[1],[0],[1],[0],[4],[0],[6],[2],[0],[1],[6],[6],[4],[4],[4],[5],[2],[2],[7],[5],[7],[4],[5],[5],[2],[3],[3],[5],[6],[7],[3],[6],[7],[4],[5],[3],[7],[5],[1],[5],[3],[6],[6],[6],[5],[2],[0],[3],[1],[2],[1],[3],[7],[4],[6],[7],[1],[2],[1],[5],[1],[2],[5],[2],[6],[4],[4],[5],[2],[6],[7],[3],[5],[0],[6],[6],[3],[6],[6],[6],[4],[5],[0],[6],[6],[4],[2],[0],[1],[7],[6],[1],[4],[7],[4],[1],[2],[5],[3],[4],[3],[0],[0],[1],[7],[3],[7],[1],[6],[4],[1],[4],[0],[6],[5],[5],[5],[6],[0],[0],[3],[7],[3],[2],[2],[6],[1],[1],[3],[0],[2],[1],[1],[6],[6],[3],[5],[4],[7],[5],[1],[5],[1],[2],[6],[5],[0],[2],[0],[1],[7],[1],[3],[5],[7],[2],[0],[2],[1],[5],[2],[2],[2],[5],[1],[0],[1],[1],[4],[1],[6],[1],[2],[1],[2],[0],[4],[0],[0],[5],[1],[3],[2],[5],[6],[5],[4],[0],[6],[0],[7],[2],[0],[1],[2],[7],[5],[5],[4],[0],[2],[4],[1],[4],[6],[0],[2],[0],[5],[5],[6],[6],[3],[5],[7],[1],[3],[4],[1],[5],[5],[4],[4],[4],[6],[6],[2],[3],[5],[3],[5],[0],[3],[3],[4],[1],[0],[0],[3],[7],[5],[7],[5],[5],[2],[0],[4],[7],[5],[4],[0],[1],[4],[3],[0],[1],[7],[6],[4],[5],[5],[2],[1],[7],[2],[6],[1],[5],[2],[2],[2],[5],[2],[4],[7],[3],[0],[7],[6],[2],[7],[1],[2],[6],[5],[7],[0],[7],[2],[6],[3],[1],[6],[3],[3],[4],[6],[7],[6],[4],[3],[6],[0],[1],[6],[1],[5],[7],[5],[2],[7],[3],[5],[3],[2],[3],[3],[3],[5],[2],[5],[4],[7],[2],[1],[6],[0],[5],[1],[2],[5],[0],[1],[4],[6],[3],[2],[4],[3],[4],[4],[4],[6],[5],[3],[1],[5],[7],[7],[4],[6],[6],[4],[6],[4],[3],[6],[1],[4],[3],[6],[1],[0],[1],[3],[1],[6],[4],[6],[3],[2],[3],[1],[0],[5],[6],[2],[5],[4],[1],[6],[3],[0],[1],[0],[5],[1],[6],[6],[5],[5],[4],[0],[5]],[[3],[6],[3],[5],[6],[7],[4],[5],[7],[5],[5],[7],[0],[4],[7],[1],[7],[7],[5],[4],[6],[3],[1],[7],[5],[0],[3],[4],[3],[7],[4],[0],[5],[6],[3],[7],[7],[1],[5],[3],[4],[5],[3],[7],[3],[3],[3],[3],[7],[1],[0],[2],[5],[3],[6],[7],[5],[6],[3],[2],[3],[7],[1],[1],[7],[5],[3],[6],[5],[7],[3],[6],[4],[1],[0],[6],[1],[5],[3],[4],[4],[1],[2],[2],[1],[5],[7],[7],[7],[6],[1],[2],[4],[2],[6],[2],[6],[3],[4],[7],[1],[0],[3],[4],[2],[4],[2],[1],[3],[0],[6],[3],[4],[4],[6],[7],[4],[0],[6],[1],[5],[3],[0],[4],[5],[2],[0],[5],[6],[4],[7],[0],[2],[0],[2],[5],[2],[4],[0],[1],[1],[7],[7],[7],[1],[5],[6],[5],[2],[5],[4],[2],[0],[6],[3],[4],[7],[7],[0],[7],[7],[0],[3],[2],[2],[2],[2],[7],[3],[4],[6],[1],[4],[0],[5],[4],[5],[5],[2],[7],[5],[6],[1],[3],[0],[4],[0],[3],[7],[0],[0],[1],[1],[5],[0],[1],[5],[3],[7],[6],[3],[0],[7],[5],[5],[3],[7],[3],[5],[2],[5],[5],[6],[6],[7],[7],[2],[6],[1],[4],[3],[7],[0],[1],[7],[2],[1],[4],[2],[1],[3],[4],[7],[3],[2],[2],[2],[0],[6],[5],[5],[0],[3],[4],[4],[5],[7],[2],[7],[5],[0],[3],[2],[5],[0],[1],[5],[2],[3],[6],[3],[5],[7],[1],[5],[1],[3],[3],[1],[4],[5],[4],[3],[6],[5],[2],[5],[1],[2],[6],[0],[5],[7],[2],[0],[1],[2],[6],[4],[7],[6],[6],[6],[4],[1],[4],[6],[2],[0],[6],[1],[3],[6],[0],[4],[5],[6],[6],[0],[6],[0],[3],[4],[2],[0],[1],[5],[1],[3],[6],[1],[6],[4],[1],[2],[7],[4],[4],[7],[4],[4],[5],[1],[5],[5],[3],[7],[0],[1],[0],[5],[5],[2],[2],[5],[4],[4],[2],[6],[2],[3],[0],[1],[5],[0],[1],[2],[3],[4],[0],[3],[5],[0],[0],[7],[5],[4],[0],[3],[5],[2],[4],[0],[3],[2],[0],[6],[0],[7],[0],[3],[2],[6],[1],[0],[7],[7],[2],[1],[5],[5],[1],[2],[0],[0],[4],[3],[1],[2],[3],[7],[4],[2],[0],[0],[4],[5],[4],[7],[5],[5],[0],[0],[2],[3],[3],[2],[0],[0],[3],[6],[1],[3],[5],[6],[4],[6],[0],[5],[7],[1],[4],[4],[5],[0],[1],[4],[4],[6],[0],[4],[6],[7],[5],[1],[6],[7],[0],[4],[1],[5],[1],[5],[2],[3],[4],[1],[4],[4],[5],[6],[0],[3],[0],[7],[7],[5],[1],[5],[7],[5],[3],[2],[0],[5],[4],[0],[2],[2],[1],[7],[3],[4],[7],[1],[4],[7],[5],[6],[7],[4],[4],[6],[2],[3],[4],[7],[3],[3],[5],[5],[5],[7],[7],[7],[0],[6],[3],[3],[1],[0],[5]],[[3],[6],[7],[5],[5],[3],[7],[7],[0],[6],[0],[0],[5],[2],[7],[7],[3],[5],[5],[3],[0],[5],[6],[4],[0],[7],[2],[1],[0],[1],[3],[6],[1],[2],[5],[2],[0],[6],[7],[5],[6],[5],[1],[2],[2],[4],[4],[2],[7],[4],[5],[3],[5],[1],[3],[6],[7],[2],[6],[7],[1],[6],[1],[6],[6],[0],[3],[0],[3],[2],[5],[4],[2],[7],[4],[4],[6],[1],[1],[1],[5],[7],[4],[5],[1],[5],[6],[6],[3],[6],[6],[3],[3],[7],[7],[5],[1],[0],[7],[5],[1],[7],[0],[7],[0],[6],[3],[4],[3],[4],[0],[6],[3],[6],[0],[6],[2],[1],[1],[6],[7],[1],[6],[6],[1],[6],[3],[4],[7],[6],[0],[1],[7],[7],[7],[2],[2],[0],[2],[2],[7],[4],[0],[0],[1],[2],[7],[7],[1],[5],[4],[2],[1],[1],[0],[2],[4],[0],[0],[3],[6],[1],[1],[5],[7],[1],[7],[4],[1],[1],[0],[4],[0],[1],[1],[1],[4],[2],[4],[0],[5],[0],[2],[7],[4],[0],[6],[6],[4],[3],[7],[3],[3],[4],[1],[1],[4],[2],[0],[5],[0],[3],[4],[5],[7],[2],[3],[0],[4],[1],[5],[7],[0],[7],[1],[5],[5],[6],[7],[5],[1],[4],[3],[2],[3],[4],[7],[7],[6],[7],[3],[7],[7],[5],[2],[7],[0],[7],[4],[3],[5],[7],[2],[3],[2],[6],[3],[7],[3],[3],[4],[5],[0],[0],[6],[0],[1],[0],[4],[7],[4],[4],[1],[5],[3],[6],[5],[4],[1],[6],[7],[0],[6],[0],[6],[6],[2],[6],[4],[4],[1],[2],[0],[5],[6],[0],[4],[2],[4],[7],[6],[4],[1],[3],[6],[7],[0],[6],[6],[6],[4],[0],[6],[6],[4],[1],[3],[1],[5],[1],[5],[0],[0],[6],[6],[6],[0],[1],[5],[1],[2],[4],[0],[7],[7],[3],[2],[5],[6],[2],[3],[7],[3],[4],[3],[0],[0],[6],[3],[0],[7],[3],[6],[7],[3],[7],[4],[4],[5],[2],[6],[6],[3],[7],[2],[0],[0],[5],[3],[5],[5],[6],[1],[2],[5],[4],[5],[4],[3],[2],[0],[4],[0],[4],[6],[7],[5],[1],[6],[7],[3],[1],[5],[4],[3],[4],[4],[4],[1],[0],[4],[1],[4],[0],[6],[2],[6],[5],[1],[6],[1],[3],[3],[2],[0],[0],[3],[4],[2],[6],[0],[4],[0],[6],[7],[2],[6],[0],[1],[1],[6],[6],[4],[7],[1],[1],[5],[7],[4],[1],[6],[2],[6],[6],[4],[4],[3],[0],[0],[7],[6],[0],[1],[3],[1],[7],[4],[1],[5],[4],[4],[2],[3],[1],[1],[7],[6],[5],[6],[7],[3],[0],[1],[3],[1],[2],[5],[7],[0],[2],[4],[5],[3],[6],[2],[1],[2],[0],[3],[6],[2],[6],[5],[6],[2],[2],[4],[7],[6],[0],[2],[4],[5],[4],[0],[4],[5],[6],[6],[2],[1],[5],[4],[7],[1],[2],[3],[2],[2],[2],[3],[2]],[[5],[6],[5],[2],[1],[5],[3],[6],[0],[6],[0],[3],[5],[0],[7],[4],[0],[3],[6],[7],[4],[1],[5],[6],[1],[7],[7],[4],[0],[2],[3],[1],[3],[7],[2],[6],[1],[6],[0],[1],[5],[6],[3],[7],[2],[2],[4],[4],[5],[1],[0],[4],[5],[1],[5],[6],[1],[1],[2],[0],[5],[4],[0],[2],[5],[0],[1],[2],[3],[6],[5],[7],[4],[3],[6],[5],[0],[4],[1],[5],[1],[4],[6],[6],[2],[6],[3],[2],[5],[6],[5],[7],[2],[1],[4],[7],[1],[6],[1],[0],[4],[6],[2],[1],[6],[3],[7],[5],[2],[2],[3],[3],[5],[4],[5],[3],[4],[0],[1],[0],[6],[0],[0],[5],[5],[7],[2],[3],[4],[2],[5],[1],[4],[5],[4],[2],[0],[0],[3],[1],[3],[2],[7],[7],[3],[0],[1],[6],[5],[1],[2],[4],[0],[5],[2],[4],[4],[7],[0],[7],[5],[0],[3],[4],[7],[0],[4],[6],[2],[4],[6],[4],[4],[5],[0],[7],[2],[3],[4],[0],[4],[3],[0],[0],[7],[7],[4],[1],[6],[7],[2],[1],[1],[3],[6],[7],[0],[7],[1],[7],[1],[2],[1],[1],[7],[4],[0],[0],[3],[4],[6],[2],[7],[6],[6],[3],[1],[7],[0],[5],[5],[0],[7],[5],[5],[6],[4],[1],[1],[5],[2],[0],[4],[6],[1],[1],[2],[6],[7],[6],[4],[4],[5],[5],[4],[5],[7],[7],[7],[7],[4],[5],[4],[0],[6],[3],[2],[0],[6],[3],[5],[1],[6],[6],[6],[7],[1],[0],[2],[4],[3],[3],[2],[1],[6],[1],[7],[6],[1],[4],[0],[2],[7],[1],[2],[6],[4],[0],[4],[6],[2],[6],[2],[3],[3],[7],[1],[2],[3],[6],[1],[2],[1],[5],[0],[0],[7],[3],[3],[6],[3],[6],[2],[1],[4],[1],[0],[2],[4],[2],[6],[0],[6],[1],[6],[7],[4],[5],[2],[1],[6],[1],[7],[5],[3],[2],[7],[5],[5],[4],[7],[4],[6],[1],[0],[3],[7],[4],[0],[6],[4],[1],[4],[3],[5],[0],[0],[7],[6],[3],[0],[2],[0],[2],[4],[0],[6],[6],[6],[7],[2],[2],[3],[4],[3],[7],[6],[4],[0],[7],[0],[1],[7],[7],[5],[3],[7],[6],[4],[6],[3],[1],[4],[6],[1],[0],[1],[6],[3],[4],[3],[3],[0],[6],[6],[2],[4],[1],[5],[6],[5],[6],[2],[0],[0],[5],[4],[1],[0],[4],[1],[4],[3],[2],[6],[3],[6],[1],[1],[6],[4],[7],[0],[1],[2],[2],[2],[1],[7],[4],[4],[5],[5],[4],[1],[4],[7],[7],[5],[2],[0],[1],[2],[0],[5],[1],[1],[3],[0],[5],[7],[1],[3],[4],[0],[4],[4],[4],[0],[6],[2],[6],[2],[5],[6],[7],[3],[3],[7],[6],[6],[3],[3],[3],[2],[5],[4],[5],[1],[6],[6],[4],[4],[6],[6],[1],[0],[0],[0],[5],[4],[0],[4],[1],[4],[1],[3],[0],[1],[4],[4],[1]]]
def setup_inputs(rng):
    return {"x": rng.standard_normal((N, 128, TOK), dtype=np.float32).astype(ml_dtypes.bfloat16), "gate": (0.5 * rng.integers(1, 4, size=(N, K, TOK)) * (2 * rng.integers(0, 2, size=(N, K, TOK)) - 1)).astype(np.float32).astype(ml_dtypes.bfloat16), "w1": (rng.standard_normal((N, 128, FT * 128), dtype=np.float32) / 8).astype(ml_dtypes.bfloat16), "w2": (rng.standard_normal((N, 128, FT * 128), dtype=np.float32) / 8).astype(ml_dtypes.bfloat16)}
def setup_inputs_big(rng):
    d = setup_inputs(rng)
    for k in ("x", "gate", "w1", "w2"): d[k] = (d[k].astype(np.float32) * 1024.0).astype(d[k].dtype)
    return d
def setup_inputs_small(rng):
    d = setup_inputs(rng)
    for k in ("x", "gate", "w1", "w2"): d[k] = (d[k].astype(np.float32) * (1 / 1024.0)).astype(d[k].dtype)
    return d
def reference(x, gate, w1, w2):
    X, GATE, W1, W2 = x.astype(np.float64), gate.astype(np.float64), w1.astype(np.float64), w2.astype(np.float64)
    y = np.zeros((N, 128, TOK))
    for r in range(N):
        for t in range(TOK):
            for i, e in enumerate(ROUTE[r][t]):
                hid = np.maximum(W1[e].T @ X[r][:, t], 0.0)
                y[r][:, t] += GATE[r][i, t] * sum(W2[e][:, 128 * f:128 * f + 128].T @ hid[128 * f:128 * f + 128] for f in range(FT))
    return {"y": y.astype(ml_dtypes.bfloat16)}

@@ -1,0 +1,264 @@
+from concourse.bass import DstId, RemoteDMATransfer
+from concourse.mybir import AluOpType
+
+NR = 8
+TOK = 512
+F = 128
+WW = 2 * F
+NB = 7
+CO = 2.0 ** 60
+
+SCRATCH = {
+    "Wall": ("sbuf", [128, NR * WW], "bfloat16"),
+    "xs": ("sbuf", [128, TOK], "bfloat16"),
+    "gs": ("sbuf", [128, TOK], "bfloat16"),
+    "ones": ("sbuf", [128, F], "bfloat16"),
+    "zeros": ("sbuf", [128, TOK], "bfloat16"),
+    "gb": ("sbuf", [128, TOK], "bfloat16"),
+    "R": ("sbuf", [128, TOK], "bfloat16"),
+    "Cb": ("sbuf", [128, NR * F], "bfloat16"),
+    "H": ("sbuf", [128, NR * TOK], "bfloat16"),
+    "ysb": ("sbuf", [128, TOK], "bfloat16"),
+    "PY": ("psum", [128, TOK], "float32"),
+}
+for _i in range(NB):
+    SCRATCH["P%d" % _i] = ("psum", [128, TOK], "float32")
+
+SEMAPHORES = ["w", "x", "g", "ms1", "msc", "msz", "gm", "gb", "r", "loc", "l2", "ya", "yb", "sta", "stb", "hms", "hsq"]
+SEMAPHORES += ["arr%d" % _i for _i in range(NR)]
+SEMAPHORES += ["l1_%d" % _i for _i in range(NR)]
+SEMAPHORES += ["rl_%d" % _i for _i in range(NR)]
+
+
+def _bits(mask):
+    return [b for b in range(32) if (mask >> b) & 1]
+
+
+def _mask(bitlist):
+    m = 0
+    for b in bitlist:
+        m |= 1 << b
+    return m
+
+
+def _cover(route, a, b):
+    out = []
+    for v in sorted(set(route[a:b])):
+        left = set(t for t in range(a, b) if route[t] == v)
+        while left:
+            pts = sorted(left)
+            best = (pts[0], 1, 1)
+            for i, s in enumerate(pts):
+                for u in pts[i + 1:]:
+                    d = u - s
+                    n = 2
+                    while s + n * d in left:
+                        n += 1
+                    if n > best[2]:
+                        best = (s, d, n)
+            for j in range(best[2]):
+                left.remove(best[0] + j * best[1])
+            out.append((v,) + best)
+    return out
+
+
+def _plan(T, topo):
+    cores = list(T.cores)
+    chips = [topo.chip(c) for c in cores]
+    n = len(cores)
+    first = sorted([r for r in range(n) if r == 0 or topo.same_plane(chips[r], chips[0])], key=lambda r: chips[r])
+    second = [[q for q in range(n) if topo.mates(chips[q], chips[r])][0] for r in first]
+    planes = [first, second]
+    hop = 1.5
+    sends, feeds, est = {}, {}, {}
+    for pl in (0, 1):
+        mine, other = planes[pl], planes[1 - pl]
+        m = len(mine)
+        for p, r in enumerate(mine):
+            c = cores[r]
+            same = [mine[(p + k) % m] for k in range(1, m)]
+            cross = [other[(p + k) % m] for k in range(m)]
+            near = [h for h in range(topo.CORES_PER_CHIP * topo.CHIPS)
+                    if topo.chip(h) == chips[r] and h != c and topo.die(h) == topo.die(c)]
+            owners = [h for h in near if topo.may_write(h, cores[cross[0]])]
+            plain = [h for h in near if h not in owners]
+            if topo.may_write(c, cores[cross[0]]):
+                a, b = owners[0], plain[0]
+                feeds[r] = [[(a, "hi")], [(b, "hi")]]
+                jobs = {c: [(same[0], 1.0), (cross[0], 2.0), (same[1], 3.0), (cross[1], 4.2)],
+                        a: [(cross[2], 2.2 + hop), (cross[3], 3.2 + hop)],
+                        b: [(same[2], 3.0 + hop)]}
+            else:
+                a, b = owners[0], owners[1]
+                feeds[r] = [[(a, "lo"), (b, "hi")]]
+                jobs = {c: [(same[0], 2.0), (same[1], 3.0), (same[2], 4.0)],
+                        a: [(cross[0], 2.0 + hop), (cross[1], 3.2 + hop)],
+                        b: [(cross[2], 2.2 + hop), (cross[3], 3.2 + hop)]}
+            for s in jobs:
+                sends[s] = [(r, q) for q, _t in jobs[s]]
+                for q, t in jobs[s]:
+                    est[(r, q)] = t
+    return {"sends": sends, "feeds": feeds, "est": est}
+
+
+def rank_program(g, core, T, topo):
+    cores = list(T.cores)
+    S = T.sem
+    chip = topo.chip(core)
+    home = [r for r in range(len(cores)) if topo.chip(cores[r]) == chip]
+    if not home:
+        return
+    r0 = home[0]
+    rc = cores[r0]
+    plan = _plan(T, topo)
+    helpers = [h for h in range(topo.CORES_PER_CHIP * topo.CHIPS) if topo.chip(h) == chip and h != rc]
+    far = [c for c in cores if topo.chip(c) != chip][0]
+    route = [e[0] for e in T.tables["ROUTE"][r0]]
+    nblk = TOK // 8
+    bounds = [0]
+    for k in range(len(helpers)):
+        bounds.append(bounds[-1] + 8 * (nblk // len(helpers) + (1 if k < nblk % len(helpers) else 0)))
+    loc = [0]
+
+    def slot(e):
+        return T.Wall[:, e * WW:(e + 1) * WW]
+
+    def put(dst, ap, sem, mask):
+        rid, pid, _se = topo.addr(dst)
+        g.remote_dma(out_ap=ap, in_ap=ap, remote_sem=sem, local_sem=S.loc, pid=pid, routing_id=rid,
+                     dma_engine_mask=mask)
+        loc[0] += len(_bits(mask))
+
+    def code_lanes(h):
+        on = topo.mask(h, rc)
+        if h in plan["sends"]:
+            return on & topo.mask(h, far)
+        return _mask(_bits(on)[:4])
+
+    def feed_mask(dst, which):
+        on, off = topo.mask(rc, dst), topo.mask(rc, far)
+        return (on & off) if which == "lo" else (on & ~off)
+
+    if core != rc:
+        k = helpers.index(core)
+        a, b = bounds[k], bounds[k + 1]
+        nms = 0
+        for v, start, step, cnt in _cover(route, a, b):
+            if cnt == 1 or step == 1:
+                ap = T.R[0:64, start:start + cnt]
+            else:
+                ap = T.R[0:64, start:start + (cnt - 1) * step + 1:step]
+            g.vector.memset(ap, float(v)).then_inc(S.hms, 1)
+            nms += 1
+        g.vector.memset(T.R[64:128, a:b], 1.0).then_inc(S.hms, 1)
+        nms += 1
+        g.vector.wait_ge(S.hms, nms)
+        g.vector.tensor_tensor(T.R[0:32, a:b], T.R[0:32, a:b], T.R[0:32, a:b], AluOpType.mult).then_inc(S.hsq, 1)
+        g.wait_ge(S.hms, nms)
+        g.wait_ge(S.hsq, 1)
+        put(rc, T.R[:, a:b], S.r, code_lanes(core))
+        jobs = plan["sends"].get(core, [])
+        if jobs:
+            which = [w for call in plan["feeds"][r0] for h, w in call if h == core][0]
+            g.wait_ge(S["arr%d" % r0], len(_bits(feed_mask(core, which))))
+            for e, q in jobs:
+                put(cores[q], slot(e), S["arr%d" % e], topo.mask(core, cores[q]))
+        g.wait_ge(S.loc, loc[0])
+        return
+
+    me = r0
+    order = [me] + sorted([e for e in range(NR) if e != me], key=lambda e: (plan["est"][(e, me)], e))
+
+    g.sync.dma_start(T.Wall[:, me * WW:me * WW + F], T.w1[:, :]).then_inc(S.w, 16)
+    g.scalar.dma_start(T.Wall[:, me * WW + F:(me + 1) * WW], T.w2[:, :]).then_inc(S.w, 16)
+    g.sync.dma_start(T.xs[:, :], T.x[:, :]).then_inc(S.x, 16)
+    g.scalar.dma_start(T.gs[0:1, :], T.gate[:, :]).then_inc(S.g, 16)
+
+    g.wait_ge(S.w, 32)
+    for call in plan["feeds"][me]:
+        if len(call) == 1:
+            h, which = call[0]
+            put(h, slot(me), S["arr%d" % me], feed_mask(h, which))
+        else:
+            trs = []
+            for h, which in call:
+                rid, pid, _se = topo.addr(h)
+                mk = feed_mask(h, which)
+                trs.append(RemoteDMATransfer(dst_ids=[DstId(rid=rid, pnc=pid)], dma_engine_mask=mk,
+                                             remote_sem=S["arr%d" % me], src=slot(me), dst=slot(me)))
+                loc[0] += len(_bits(mk))
+            g.remote_dma_fused(trs, local_sem=S.loc)
+    for e, q in plan["sends"][core]:
+        put(cores[q], slot(e), S["arr%d" % e], topo.mask(core, cores[q]))
+    g.wait_ge(S.loc, loc[0])
+
+    V = g.vector
+    V.memset(T.ones[0:1, :], 1.0).then_inc(S.ms1, 1)
+    nc = 0
+    V.memset(T.Cb[0:32, :], -CO).then_inc(S.msc, 1)
+    V.memset(T.Cb[96:128, :], 0.0).then_inc(S.msc, 1)
+    nc += 2
+    for e in range(NR):
+        V.memset(T.Cb[32:64, e * F:(e + 1) * F], 2.0 * e * CO).then_inc(S.msc, 1)
+        V.memset(T.Cb[64:96, e * F:(e + 1) * F], -1.0 * e * e * CO).then_inc(S.msc, 1)
+        nc += 2
+    V.memset(T.zeros[:, :], 0.0).then_inc(S.msz, 1)
+    V.wait_ge(S.gm, 1)
+    V.tensor_copy(T.gb[:, :], T.PY[:, :]).then_inc(S.gb, 1)
+    V.wait_ge(S.msz, 1)
+    for j in range(NR):
+        V.wait_ge(S["l1_%d" % j], 1)
+        V.tensor_tensor(T.H[:, j * TOK:(j + 1) * TOK], T["P%d" % (j % NB)][:, :], T.zeros[:, :],
+                        AluOpType.max).then_inc(S["rl_%d" % j], 1)
+    V.wait_ge(S.l2, NR)
+    V.wait_ge(S.gb, 1)
+    hf = TOK // 2
+    V.tensor_tensor(T.ysb[:, 0:hf], T.PY[:, 0:hf], T.gb[:, 0:hf], AluOpType.mult).then_inc(S.ya, 1)
+    V.tensor_tensor(T.ysb[:, hf:TOK], T.PY[:, hf:TOK], T.gb[:, hf:TOK], AluOpType.mult).then_inc(S.yb, 1)
+
+    P = g.tensor
+    n_r = sum(len(_bits(code_lanes(h))) for h in helpers)
+
+    def w1(e):
+        return T.Wall[:, e * WW:e * WW + F]
+
+    def w2(e):
+        return T.Wall[:, e * WW + F:(e + 1) * WW]
+
+    def bias(j, start, stop):
+        e = order[j]
+        return P.matmul(T["P%d" % (j % NB)][:, :], T.Cb[:, e * F:(e + 1) * F], T.R[:, :], start=start, stop=stop)
+
+    def second(j):
+        P.wait_ge(S["rl_%d" % j], 1)
+        P.matmul(T.PY[:, :], w2(order[j]), T.H[:, j * TOK:(j + 1) * TOK], start=(j == 0),
+                 stop=(j == NR - 1)).then_inc(S.l2, 1)
+
+    P.wait_ge(S.ms1, 1)
+    P.wait_ge(S.g, 16)
+    P.matmul(T.PY[:, :], T.ones[0:1, :], T.gs[0:1, :], start=True, stop=True).then_inc(S.gm, 1)
+    P.wait_ge(S.w, 32)
+    P.wait_ge(S.x, 16)
+    P.matmul(T.P0[:, :], w1(me), T.xs[:, :], start=True, stop=False)
+    P.wait_ge(S.msc, nc)
+    P.wait_ge(S.r, n_r)
+    bias(0, False, True).then_inc(S.l1_0, 1)
+    for j in range(1, NB):
+        bias(j, True, False)
+    P.wait_ge(S.gb, 1)
+    for j in range(1, NR):
+        e = order[j]
+        src_n = len(_bits(topo.mask(cores[e], core)))
+        P.wait_ge(S["arr%d" % e], src_n)
+        P.matmul(T["P%d" % (j % NB)][:, :], w1(e), T.xs[:, :], start=False, stop=True).then_inc(S["l1_%d" % j], 1)
+        second(j - 1)
+        if j - 1 + NB < NR:
+            bias(j - 1 + NB, True, False)
+    second(NR - 1)
+
+    g.sync.wait_ge(S.ya, 1)
+    g.sync.dma_start(T.y[:, 0:hf], T.ysb[:, 0:hf]).then_inc(S.sta, 16)
+    g.sync.wait_ge(S.sta, 16)
+    g.scalar.wait_ge(S.yb, 1)
+    g.scalar.dma_start(T.y[:, hf:TOK], T.ysb[:, hf:TOK]).then_inc(S.stb, 16)
+    g.scalar.wait_ge(S.stb, 16)

@@ -3,9 +3,12 @@ from concourse.mybir import AluOpType
 
 NR = 8
 TOK = 512
+HF = TOK // 2
 F = 128
 WW = 2 * F
-NB = 7
+NB = 6
+HEAD = 8
+GROUP = (1, 2, 3)
 CO = 2.0 ** 60
 
 SCRATCH = {
@@ -19,15 +22,21 @@ SCRATCH = {
     "Cb": ("sbuf", [128, NR * F], "bfloat16"),
     "H": ("sbuf", [128, NR * TOK], "bfloat16"),
     "ysb": ("sbuf", [128, TOK], "bfloat16"),
-    "PY": ("psum", [128, TOK], "float32"),
+    "YB": ("sbuf", [128, TOK], "bfloat16"),
+    "D1": ("sbuf", [128, F + 1], "bfloat16"),
+    "Dd": ("dram", [F + 1, 128], "bfloat16"),
+    "I": ("sbuf", [128, F], "bfloat16"),
+    "Y0": ("psum", [128, TOK], "float32"),
+    "Y1": ("psum", [128, TOK], "float32"),
 }
 for _i in range(NB):
     SCRATCH["P%d" % _i] = ("psum", [128, TOK], "float32")
 
-SEMAPHORES = ["w", "x", "g", "ms1", "msc", "msz", "gm", "gb", "r", "loc", "l2", "ya", "yb", "sta", "stb", "hms", "hsq"]
+SEMAPHORES = ["w", "x", "g", "ms1", "msc", "msb", "msz", "gm", "gb", "r", "loc", "l2_0", "l2_1", "y0", "y1", "st0",
+              "st1", "hms0", "hms1", "hsq0", "hsq1", "xr", "cbr", "pb0", "pb1", "id0", "id1", "id2"]
 SEMAPHORES += ["arr%d" % _i for _i in range(NR)]
-SEMAPHORES += ["l1_%d" % _i for _i in range(NR)]
-SEMAPHORES += ["rl_%d" % _i for _i in range(NR)]
+SEMAPHORES += ["l1_%d" % _i for _i in range(NR + 1)]
+SEMAPHORES += ["rl_%d" % _i for _i in range(NR + 1)]
 
 
 def _bits(mask):
@@ -66,6 +75,7 @@ def _plan(T, topo):
     cores = list(T.cores)
     chips = [topo.chip(c) for c in cores]
     n = len(cores)
+    every = range(topo.CORES_PER_CHIP * topo.CHIPS)
     first = sorted([r for r in range(n) if r == 0 or topo.same_plane(chips[r], chips[0])], key=lambda r: chips[r])
     second = [[q for q in range(n) if topo.mates(chips[q], chips[r])][0] for r in first]
     planes = [first, second]
@@ -78,8 +88,7 @@ def _plan(T, topo):
             c = cores[r]
             same = [mine[(p + k) % m] for k in range(1, m)]
             cross = [other[(p + k) % m] for k in range(m)]
-            near = [h for h in range(topo.CORES_PER_CHIP * topo.CHIPS)
-                    if topo.chip(h) == chips[r] and h != c and topo.die(h) == topo.die(c)]
+            near = [h for h in every if topo.chip(h) == chips[r] and h != c and topo.die(h) == topo.die(c)]
             owners = [h for h in near if topo.may_write(h, cores[cross[0]])]
             plain = [h for h in near if h not in owners]
             if topo.may_write(c, cores[cross[0]]):
@@ -98,7 +107,15 @@ def _plan(T, topo):
                 sends[s] = [(r, q) for q, _t in jobs[s]]
                 for q, t in jobs[s]:
                     est[(r, q)] = t
-    return {"sends": sends, "feeds": feeds, "est": est}
+    order, bcore, land = {}, {}, {}
+    for q in range(n):
+        order[q] = [q] + sorted([e for e in range(n) if e != q], key=lambda e: (est[(e, q)], e))
+        free = [h for h in every if topo.chip(h) == chips[q] and h != cores[q] and h not in sends]
+        free.sort(key=lambda h: (topo.die(h) != topo.die(cores[q]), h))
+        bcore[q] = free[0]
+        for i, e in enumerate(order[q]):
+            land[(e, q)] = bcore[q] if i in GROUP else cores[q]
+    return {"sends": sends, "feeds": feeds, "order": order, "bcore": bcore, "land": land}
 
 
 def rank_program(g, core, T, topo):
@@ -111,69 +128,158 @@ def rank_program(g, core, T, topo):
     r0 = home[0]
     rc = cores[r0]
     plan = _plan(T, topo)
+    bc = plan["bcore"][r0]
     helpers = [h for h in range(topo.CORES_PER_CHIP * topo.CHIPS) if topo.chip(h) == chip and h != rc]
     far = [c for c in cores if topo.chip(c) != chip][0]
     route = [e[0] for e in T.tables["ROUTE"][r0]]
+    seq_b = [plan["order"][r0][i] for i in GROUP]
+    seq = [e for i, e in enumerate(plan["order"][r0]) if i not in GROUP]
     nblk = TOK // 8
     bounds = [0]
     for k in range(len(helpers)):
         bounds.append(bounds[-1] + 8 * (nblk // len(helpers) + (1 if k < nblk % len(helpers) else 0)))
     loc = [0]
+    V = g.vector
+    P = g.tensor
 
     def slot(e):
         return T.Wall[:, e * WW:(e + 1) * WW]
 
-    def put(dst, ap, sem, mask):
+    def put(dst, ap, sem, mask, out=None):
         rid, pid, _se = topo.addr(dst)
-        g.remote_dma(out_ap=ap, in_ap=ap, remote_sem=sem, local_sem=S.loc, pid=pid, routing_id=rid,
-                     dma_engine_mask=mask)
+        g.remote_dma(out_ap=(ap if out is None else out), in_ap=ap, remote_sem=sem, local_sem=S.loc, pid=pid,
+                     routing_id=rid, dma_engine_mask=mask)
         loc[0] += len(_bits(mask))
 
     def code_lanes(h):
         on = topo.mask(h, rc)
         if h in plan["sends"]:
             return on & topo.mask(h, far)
+        if h == bc:
+            return on
         return _mask(_bits(on)[:4])
 
     def feed_mask(dst, which):
         on, off = topo.mask(rc, dst), topo.mask(rc, far)
         return (on & off) if which == "lo" else (on & ~off)
 
+    def ship(e, q):
+        dst = plan["land"][(e, q)]
+        put(dst, slot(e), S["arr%d" % e], topo.mask(core, dst))
+
+    def w1(e):
+        return T.Wall[:, e * WW:e * WW + F]
+
+    def w2(e):
+        return T.Wall[:, e * WW + F:(e + 1) * WW]
+
+    def coeffs(experts, base, sem):
+        n = len(experts)
+        V.memset(T.Cb[0:32, base * F:(base + n) * F], -CO).then_inc(sem, 1)
+        V.memset(T.Cb[96:128, base * F:(base + n) * F], 0.0).then_inc(sem, 1)
+        for j, e in enumerate(experts):
+            V.memset(T.Cb[32:64, (base + j) * F:(base + j + 1) * F], 2.0 * e * CO).then_inc(sem, 1)
+            V.memset(T.Cb[64:96, (base + j) * F:(base + j + 1) * F], -1.0 * e * e * CO).then_inc(sem, 1)
+        return 2 + 2 * n
+
+    def n_arr(e):
+        return len(_bits(topo.mask(cores[e], core)))
+
     if core != rc:
         k = helpers.index(core)
         a, b = bounds[k], bounds[k + 1]
-        nms = 0
-        for v, start, step, cnt in _cover(route, a, b):
-            if cnt == 1 or step == 1:
-                ap = T.R[0:64, start:start + cnt]
-            else:
-                ap = T.R[0:64, start:start + (cnt - 1) * step + 1:step]
-            g.vector.memset(ap, float(v)).then_inc(S.hms, 1)
-            nms += 1
-        g.vector.memset(T.R[64:128, a:b], 1.0).then_inc(S.hms, 1)
-        nms += 1
-        g.vector.wait_ge(S.hms, nms)
-        g.vector.tensor_tensor(T.R[0:32, a:b], T.R[0:32, a:b], T.R[0:32, a:b], AluOpType.mult).then_inc(S.hsq, 1)
-        g.wait_ge(S.hms, nms)
-        g.wait_ge(S.hsq, 1)
-        put(rc, T.R[:, a:b], S.r, code_lanes(core))
+        pieces = [(a, a + HEAD), (a + HEAD, b)]
+        counts = []
+        for i, (pa, pb) in enumerate(pieces):
+            nms = 1
+            V.memset(T.R[64:128, pa:pb], 1.0).then_inc(S["hms%d" % i], 1)
+            for v, start, step, cnt in _cover(route, pa, pb):
+                if cnt == 1 or step == 1:
+                    ap = T.R[0:64, start:start + cnt]
+                else:
+                    ap = T.R[0:64, start:start + (cnt - 1) * step + 1:step]
+                V.memset(ap, float(v)).then_inc(S["hms%d" % i], 1)
+                nms += 1
+            counts.append(nms)
+            V.wait_ge(S["hms%d" % i], nms)
+            V.tensor_tensor(T.R[0:32, pa:pb], T.R[0:32, pa:pb], T.R[0:32, pa:pb],
+                            AluOpType.mult).then_inc(S["hsq%d" % i], 1)
+            g.wait_ge(S["hms%d" % i], nms)
+            g.wait_ge(S["hsq%d" % i], 1)
+            put(rc, T.R[:, pa:pb], S.r, code_lanes(core))
+            if core != bc:
+                put(bc, T.R[:, pa:pb], S.r, code_lanes(core))
         jobs = plan["sends"].get(core, [])
         if jobs:
             which = [w for call in plan["feeds"][r0] for h, w in call if h == core][0]
             g.wait_ge(S["arr%d" % r0], len(_bits(feed_mask(core, which))))
             for e, q in jobs:
-                put(cores[q], slot(e), S["arr%d" % e], topo.mask(core, cores[q]))
+                ship(e, q)
+        if core == bc:
+            n = len(seq_b)
+            V.memset(T.zeros[:, :], 0.0).then_inc(S.msz, 1)
+            V.wait_ge(S.msz, 1)
+            for j in range(n):
+                V.wait_ge(S["l1_%d" % j], 1)
+                V.tensor_tensor(T.H[:, j * TOK:(j + 1) * TOK], T["P%d" % j][:, :], T.zeros[:, :],
+                                AluOpType.max).then_inc(S["rl_%d" % j], 1)
+            for h in (0, 1):
+                V.wait_ge(S["l2_%d" % h], n)
+                V.tensor_copy(T.ysb[:, h * HF:(h + 1) * HF], T["Y%d" % h][:, 0:HF]).then_inc(S["y%d" % h], 1)
+
+            def sec(j):
+                P.wait_ge(S["rl_%d" % j], 1)
+                for h in (0, 1):
+                    P.matmul(T["Y%d" % h][:, 0:HF], w2(seq_b[j]), T.H[:, j * TOK + h * HF:j * TOK + (h + 1) * HF],
+                             start=(j == 0), stop=(j == n - 1)).then_inc(S["l2_%d" % h], 1)
+
+            P.wait_ge(S.cbr, len(_bits(topo.mask(rc, bc))))
+            for i in (0, 1):
+                P.wait_ge(S["hms%d" % i], counts[i])
+                P.wait_ge(S["hsq%d" % i], 1)
+            P.wait_ge(S.r, 2 * sum(len(_bits(code_lanes(h))) for h in helpers if h != bc))
+            for j in range(n):
+                P.matmul(T["P%d" % j][:, :], T.Cb[:, j * F:(j + 1) * F], T.R[:, :], start=True, stop=False)
+            P.wait_ge(S.xr, len(_bits(feed_mask(bc, "hi"))))
+            for j in range(n):
+                P.wait_ge(S["arr%d" % seq_b[j]], n_arr(seq_b[j]))
+                P.matmul(T["P%d" % j][:, :], w1(seq_b[j]), T.xs[:, :], start=False,
+                         stop=True).then_inc(S["l1_%d" % j], 1)
+                if j >= 1:
+                    sec(j - 1)
+            sec(n - 1)
+            for h in (0, 1):
+                g.wait_ge(S["y%d" % h], 1)
+                put(rc, T.ysb[:, h * HF:(h + 1) * HF], S["pb%d" % h], topo.mask(core, rc),
+                    out=T.YB[:, h * HF:(h + 1) * HF])
         g.wait_ge(S.loc, loc[0])
         return
 
     me = r0
-    order = [me] + sorted([e for e in range(NR) if e != me], key=lambda e: (plan["est"][(e, me)], e))
+    n = len(seq)
+    nb = len(seq_b)
+    LAST = n - 1
+    LB = [LAST % NB, (LAST + 1) % NB]
+    LS = NR - 1
 
     g.sync.dma_start(T.Wall[:, me * WW:me * WW + F], T.w1[:, :]).then_inc(S.w, 16)
     g.scalar.dma_start(T.Wall[:, me * WW + F:(me + 1) * WW], T.w2[:, :]).then_inc(S.w, 16)
     g.sync.dma_start(T.xs[:, :], T.x[:, :]).then_inc(S.x, 16)
     g.scalar.dma_start(T.gs[0:1, :], T.gate[:, :]).then_inc(S.g, 16)
+    g.sync.wait_ge(S.id0, 2)
+    g.sync.dma_start(T.Dd[:, :], T.D1[:, :]).then_inc(S.id1, 16)
+    g.sync.wait_ge(S.id1, 16)
+    g.sync.dma_start(T.I[:, :], T.Dd[0:128, :]).then_inc(S.id2, 16)
 
+    ncb = coeffs(seq_b, n, S.msb)
+    V.memset(T.ones[0:1, :], 1.0).then_inc(S.ms1, 1)
+    nc = coeffs(seq, 0, S.msc)
+    V.memset(T.zeros[:, :], 0.0).then_inc(S.msz, 1)
+    V.memset(T.D1[:, 0:1], 1.0).then_inc(S.id0, 1)
+    V.memset(T.D1[:, 1:F + 1], 0.0).then_inc(S.id0, 1)
+
+    g.wait_ge(S.msb, ncb)
+    put(bc, T.Cb[:, n * F:(n + nb) * F], S.cbr, topo.mask(rc, bc), out=T.Cb[:, 0:nb * F])
     g.wait_ge(S.w, 32)
     for call in plan["feeds"][me]:
         if len(call) == 1:
@@ -188,77 +294,87 @@ def rank_program(g, core, T, topo):
                                              remote_sem=S["arr%d" % me], src=slot(me), dst=slot(me)))
                 loc[0] += len(_bits(mk))
             g.remote_dma_fused(trs, local_sem=S.loc)
+    g.wait_ge(S.x, 16)
+    put(bc, T.xs[:, :], S.xr, feed_mask(bc, "hi"))
     for e, q in plan["sends"][core]:
-        put(cores[q], slot(e), S["arr%d" % e], topo.mask(core, cores[q]))
+        ship(e, q)
     g.wait_ge(S.loc, loc[0])
 
-    V = g.vector
-    V.memset(T.ones[0:1, :], 1.0).then_inc(S.ms1, 1)
-    nc = 0
-    V.memset(T.Cb[0:32, :], -CO).then_inc(S.msc, 1)
-    V.memset(T.Cb[96:128, :], 0.0).then_inc(S.msc, 1)
-    nc += 2
-    for e in range(NR):
-        V.memset(T.Cb[32:64, e * F:(e + 1) * F], 2.0 * e * CO).then_inc(S.msc, 1)
-        V.memset(T.Cb[64:96, e * F:(e + 1) * F], -1.0 * e * e * CO).then_inc(S.msc, 1)
-        nc += 2
-    V.memset(T.zeros[:, :], 0.0).then_inc(S.msz, 1)
     V.wait_ge(S.gm, 1)
-    V.tensor_copy(T.gb[:, :], T.PY[:, :]).then_inc(S.gb, 1)
+    V.tensor_copy(T.gb[:, :], T.Y0[:, :]).then_inc(S.gb, 1)
     V.wait_ge(S.msz, 1)
-    for j in range(NR):
+    for j in range(LAST):
         V.wait_ge(S["l1_%d" % j], 1)
-        V.tensor_tensor(T.H[:, j * TOK:(j + 1) * TOK], T["P%d" % (j % NB)][:, :], T.zeros[:, :],
+        V.tensor_tensor(T.H[:, j * TOK:(j + 1) * TOK], T["P%d" % j][:, :], T.zeros[:, :],
                         AluOpType.max).then_inc(S["rl_%d" % j], 1)
-    V.wait_ge(S.l2, NR)
+    for h in (0, 1):
+        V.wait_ge(S["l1_%d" % (LS + h)], 1)
+        V.tensor_tensor(T.H[:, LAST * TOK + h * HF:LAST * TOK + (h + 1) * HF], T["P%d" % LB[h]][:, 0:HF],
+                        T.zeros[:, 0:HF], AluOpType.max).then_inc(S["rl_%d" % (LS + h)], 1)
     V.wait_ge(S.gb, 1)
-    hf = TOK // 2
-    V.tensor_tensor(T.ysb[:, 0:hf], T.PY[:, 0:hf], T.gb[:, 0:hf], AluOpType.mult).then_inc(S.ya, 1)
-    V.tensor_tensor(T.ysb[:, hf:TOK], T.PY[:, hf:TOK], T.gb[:, hf:TOK], AluOpType.mult).then_inc(S.yb, 1)
+    for h in (0, 1):
+        V.wait_ge(S["l2_%d" % h], n + 1)
+        V.tensor_tensor(T.ysb[:, h * HF:(h + 1) * HF], T["Y%d" % h][:, 0:HF], T.gb[:, h * HF:(h + 1) * HF],
+                        AluOpType.mult).then_inc(S["y%d" % h], 1)
 
-    P = g.tensor
-    n_r = sum(len(_bits(code_lanes(h))) for h in helpers)
+    n_r = 2 * sum(len(_bits(code_lanes(h))) for h in helpers)
 
-    def w1(e):
-        return T.Wall[:, e * WW:e * WW + F]
+    def cb(j):
+        return T.Cb[:, j * F:(j + 1) * F]
 
-    def w2(e):
-        return T.Wall[:, e * WW + F:(e + 1) * WW]
+    def second(j, h):
+        P.matmul(T["Y%d" % h][:, 0:HF], w2(seq[j]), T.H[:, j * TOK + h * HF:j * TOK + (h + 1) * HF], start=(j == 0),
+                 stop=(j == LAST)).then_inc(S["l2_%d" % h], 1)
 
-    def bias(j, start, stop):
-        e = order[j]
-        return P.matmul(T["P%d" % (j % NB)][:, :], T.Cb[:, e * F:(e + 1) * F], T.R[:, :], start=start, stop=stop)
-
-    def second(j):
-        P.wait_ge(S["rl_%d" % j], 1)
-        P.matmul(T.PY[:, :], w2(order[j]), T.H[:, j * TOK:(j + 1) * TOK], start=(j == 0),
-                 stop=(j == NR - 1)).then_inc(S.l2, 1)
+    def last_bias(h):
+        P.matmul(T["P%d" % LB[h]][:, 0:HF], cb(LAST), T.R[:, h * HF:(h + 1) * HF], start=True, stop=False)
 
     P.wait_ge(S.ms1, 1)
     P.wait_ge(S.g, 16)
-    P.matmul(T.PY[:, :], T.ones[0:1, :], T.gs[0:1, :], start=True, stop=True).then_inc(S.gm, 1)
+    P.matmul(T.Y0[:, :], T.ones[0:1, :], T.gs[0:1, :], start=True, stop=True).then_inc(S.gm, 1)
     P.wait_ge(S.w, 32)
     P.wait_ge(S.x, 16)
     P.matmul(T.P0[:, :], w1(me), T.xs[:, :], start=True, stop=False)
     P.wait_ge(S.msc, nc)
     P.wait_ge(S.r, n_r)
-    bias(0, False, True).then_inc(S.l1_0, 1)
-    for j in range(1, NB):
-        bias(j, True, False)
+    P.matmul(T.P0[:, :], cb(0), T.R[:, :], start=False, stop=True).then_inc(S.l1_0, 1)
+    for j in range(1, LAST):
+        P.matmul(T["P%d" % j][:, :], cb(j), T.R[:, :], start=True, stop=False)
+    for h in (0, 1):
+        if LB[h] != 0:
+            last_bias(h)
     P.wait_ge(S.gb, 1)
-    for j in range(1, NR):
-        e = order[j]
-        src_n = len(_bits(topo.mask(cores[e], core)))
-        P.wait_ge(S["arr%d" % e], src_n)
-        P.matmul(T["P%d" % (j % NB)][:, :], w1(e), T.xs[:, :], start=False, stop=True).then_inc(S["l1_%d" % j], 1)
-        second(j - 1)
-        if j - 1 + NB < NR:
-            bias(j - 1 + NB, True, False)
-    second(NR - 1)
+    P.wait_ge(S.rl_0, 1)
+    second(0, 0)
+    second(0, 1)
+    for h in (0, 1):
+        if LB[h] == 0:
+            last_bias(h)
+    for j in range(1, n):
+        e = seq[j]
+        P.wait_ge(S["arr%d" % e], n_arr(e))
+        if j < LAST:
+            P.matmul(T["P%d" % j][:, :], w1(e), T.xs[:, :], start=False, stop=True).then_inc(S["l1_%d" % j], 1)
+        else:
+            for h in (0, 1):
+                P.matmul(T["P%d" % LB[h]][:, 0:HF], w1(e), T.xs[:, h * HF:(h + 1) * HF], start=False,
+                         stop=True).then_inc(S["l1_%d" % (LS + h)], 1)
+        if j >= 2:
+            P.wait_ge(S["rl_%d" % (j - 1)], 1)
+            second(j - 1, 0)
+            second(j - 1, 1)
+    P.wait_ge(S.id2, 16)
+    for h in (0, 1):
+        P.wait_ge(S["pb%d" % h], len(_bits(topo.mask(bc, rc))))
+        P.matmul(T["Y%d" % h][:, 0:HF], T.I[:, :], T.YB[:, h * HF:(h + 1) * HF], start=False,
+                 stop=False).then_inc(S["l2_%d" % h], 1)
+    for h in (0, 1):
+        P.wait_ge(S["rl_%d" % (LS + h)], 1)
+        second(LAST, h)
 
-    g.sync.wait_ge(S.ya, 1)
-    g.sync.dma_start(T.y[:, 0:hf], T.ysb[:, 0:hf]).then_inc(S.sta, 16)
-    g.sync.wait_ge(S.sta, 16)
-    g.scalar.wait_ge(S.yb, 1)
-    g.scalar.dma_start(T.y[:, hf:TOK], T.ysb[:, hf:TOK]).then_inc(S.stb, 16)
-    g.scalar.wait_ge(S.stb, 16)
+    g.sync.wait_ge(S.y0, 1)
+    g.sync.dma_start(T.y[:, 0:HF], T.ysb[:, 0:HF]).then_inc(S.st0, 16)
+    g.sync.wait_ge(S.st0, 16)
+    g.scalar.wait_ge(S.y1, 1)
+    g.scalar.dma_start(T.y[:, HF:TOK], T.ysb[:, HF:TOK]).then_inc(S.st1, 16)
+    g.scalar.wait_ge(S.st1, 16)

@@ -93,10 +93,10 @@ def _plan(T, topo):
             plain = [h for h in near if h not in owners]
             if topo.may_write(c, cores[cross[0]]):
                 a, b = owners[0], plain[0]
-                feeds[r] = [[(a, "hi")], [(b, "hi")]]
-                jobs = {c: [(same[0], 1.0), (cross[0], 2.0), (same[1], 3.0), (cross[1], 4.2)],
+                feeds[r] = [[(a, "lo"), (b, "hi")]]
+                jobs = {c: [(same[0], 2.0), (cross[0], 3.0), (cross[1], 4.2)],
                         a: [(cross[2], 2.2 + hop), (cross[3], 3.2 + hop)],
-                        b: [(same[2], 3.0 + hop)]}
+                        b: [(same[1], 2.0 + hop), (same[2], 3.0 + hop)]}
             else:
                 a, b = owners[0], owners[1]
                 feeds[r] = [[(a, "lo"), (b, "hi")]]
@@ -141,6 +141,7 @@ def rank_program(g, core, T, topo):
     loc = [0]
     V = g.vector
     P = g.tensor
+    LS = NR - 1
 
     def slot(e):
         return T.Wall[:, e * WW:(e + 1) * WW]
@@ -176,11 +177,10 @@ def rank_program(g, core, T, topo):
     def coeffs(experts, base, sem):
         n = len(experts)
         V.memset(T.Cb[0:32, base * F:(base + n) * F], -CO).then_inc(sem, 1)
-        V.memset(T.Cb[96:128, base * F:(base + n) * F], 0.0).then_inc(sem, 1)
         for j, e in enumerate(experts):
             V.memset(T.Cb[32:64, (base + j) * F:(base + j + 1) * F], 2.0 * e * CO).then_inc(sem, 1)
-            V.memset(T.Cb[64:96, (base + j) * F:(base + j + 1) * F], -1.0 * e * e * CO).then_inc(sem, 1)
-        return 2 + 2 * n
+            V.memset(T.Cb[64:128, (base + j) * F:(base + j + 1) * F], -0.5 * e * e * CO).then_inc(sem, 1)
+        return 1 + 2 * n
 
     def n_arr(e):
         return len(_bits(topo.mask(cores[e], core)))
@@ -217,37 +217,54 @@ def rank_program(g, core, T, topo):
                 ship(e, q)
         if core == bc:
             n = len(seq_b)
+            LQ = n - 1
             V.memset(T.zeros[:, :], 0.0).then_inc(S.msz, 1)
+            nown = coeffs(seq_b[1:], 1, S.msc)
             V.wait_ge(S.msz, 1)
-            for j in range(n):
+            for j in range(LQ):
                 V.wait_ge(S["l1_%d" % j], 1)
                 V.tensor_tensor(T.H[:, j * TOK:(j + 1) * TOK], T["P%d" % j][:, :], T.zeros[:, :],
                                 AluOpType.max).then_inc(S["rl_%d" % j], 1)
             for h in (0, 1):
+                V.wait_ge(S["l1_%d" % (LS + h)], 1)
+                V.tensor_tensor(T.H[:, LQ * TOK + h * HF:LQ * TOK + (h + 1) * HF], T["P%d" % (LQ + h)][:, 0:HF],
+                                T.zeros[:, 0:HF], AluOpType.max).then_inc(S["rl_%d" % (LS + h)], 1)
+            for h in (0, 1):
                 V.wait_ge(S["l2_%d" % h], n)
                 V.tensor_copy(T.ysb[:, h * HF:(h + 1) * HF], T["Y%d" % h][:, 0:HF]).then_inc(S["y%d" % h], 1)
 
-            def sec(j):
-                P.wait_ge(S["rl_%d" % j], 1)
-                for h in (0, 1):
-                    P.matmul(T["Y%d" % h][:, 0:HF], w2(seq_b[j]), T.H[:, j * TOK + h * HF:j * TOK + (h + 1) * HF],
-                             start=(j == 0), stop=(j == n - 1)).then_inc(S["l2_%d" % h], 1)
+            def sec(j, h):
+                P.matmul(T["Y%d" % h][:, 0:HF], w2(seq_b[j]), T.H[:, j * TOK + h * HF:j * TOK + (h + 1) * HF],
+                         start=(j == 0), stop=(j == n - 1)).then_inc(S["l2_%d" % h], 1)
 
             P.wait_ge(S.cbr, len(_bits(topo.mask(rc, bc))))
+            P.wait_ge(S.msc, nown)
             for i in (0, 1):
                 P.wait_ge(S["hms%d" % i], counts[i])
                 P.wait_ge(S["hsq%d" % i], 1)
             P.wait_ge(S.r, 2 * sum(len(_bits(code_lanes(h))) for h in helpers if h != bc))
-            for j in range(n):
+            for j in range(LQ):
                 P.matmul(T["P%d" % j][:, :], T.Cb[:, j * F:(j + 1) * F], T.R[:, :], start=True, stop=False)
+            for h in (0, 1):
+                P.matmul(T["P%d" % (LQ + h)][:, 0:HF], T.Cb[:, LQ * F:(LQ + 1) * F], T.R[:, h * HF:(h + 1) * HF],
+                         start=True, stop=False)
             P.wait_ge(S.xr, len(_bits(feed_mask(bc, "hi"))))
             for j in range(n):
                 P.wait_ge(S["arr%d" % seq_b[j]], n_arr(seq_b[j]))
-                P.matmul(T["P%d" % j][:, :], w1(seq_b[j]), T.xs[:, :], start=False,
-                         stop=True).then_inc(S["l1_%d" % j], 1)
+                if j < LQ:
+                    P.matmul(T["P%d" % j][:, :], w1(seq_b[j]), T.xs[:, :], start=False,
+                             stop=True).then_inc(S["l1_%d" % j], 1)
+                else:
+                    for h in (0, 1):
+                        P.matmul(T["P%d" % (LQ + h)][:, 0:HF], w1(seq_b[j]), T.xs[:, h * HF:(h + 1) * HF],
+                                 start=False, stop=True).then_inc(S["l1_%d" % (LS + h)], 1)
                 if j >= 1:
-                    sec(j - 1)
-            sec(n - 1)
+                    P.wait_ge(S["rl_%d" % (j - 1)], 1)
+                    sec(j - 1, 0)
+                    sec(j - 1, 1)
+            for h in (0, 1):
+                P.wait_ge(S["rl_%d" % (LS + h)], 1)
+                sec(LQ, h)
             for h in (0, 1):
                 g.wait_ge(S["y%d" % h], 1)
                 put(rc, T.ysb[:, h * HF:(h + 1) * HF], S["pb%d" % h], topo.mask(core, rc),
@@ -257,10 +274,8 @@ def rank_program(g, core, T, topo):
 
     me = r0
     n = len(seq)
-    nb = len(seq_b)
     LAST = n - 1
     LB = [LAST % NB, (LAST + 1) % NB]
-    LS = NR - 1
 
     g.sync.dma_start(T.Wall[:, me * WW:me * WW + F], T.w1[:, :]).then_inc(S.w, 16)
     g.scalar.dma_start(T.Wall[:, me * WW + F:(me + 1) * WW], T.w2[:, :]).then_inc(S.w, 16)
@@ -271,7 +286,7 @@ def rank_program(g, core, T, topo):
     g.sync.wait_ge(S.id1, 16)
     g.sync.dma_start(T.I[:, :], T.Dd[0:128, :]).then_inc(S.id2, 16)
 
-    ncb = coeffs(seq_b, n, S.msb)
+    ncb = coeffs(seq_b[:1], n, S.msb)
     V.memset(T.ones[0:1, :], 1.0).then_inc(S.ms1, 1)
     nc = coeffs(seq, 0, S.msc)
     V.memset(T.zeros[:, :], 0.0).then_inc(S.msz, 1)
@@ -279,21 +294,17 @@ def rank_program(g, core, T, topo):
     V.memset(T.D1[:, 1:F + 1], 0.0).then_inc(S.id0, 1)
 
     g.wait_ge(S.msb, ncb)
-    put(bc, T.Cb[:, n * F:(n + nb) * F], S.cbr, topo.mask(rc, bc), out=T.Cb[:, 0:nb * F])
+    put(bc, T.Cb[:, n * F:(n + 1) * F], S.cbr, topo.mask(rc, bc), out=T.Cb[:, 0:F])
     g.wait_ge(S.w, 32)
     for call in plan["feeds"][me]:
-        if len(call) == 1:
-            h, which = call[0]
-            put(h, slot(me), S["arr%d" % me], feed_mask(h, which))
-        else:
-            trs = []
-            for h, which in call:
-                rid, pid, _se = topo.addr(h)
-                mk = feed_mask(h, which)
-                trs.append(RemoteDMATransfer(dst_ids=[DstId(rid=rid, pnc=pid)], dma_engine_mask=mk,
-                                             remote_sem=S["arr%d" % me], src=slot(me), dst=slot(me)))
-                loc[0] += len(_bits(mk))
-            g.remote_dma_fused(trs, local_sem=S.loc)
+        trs = []
+        for h, which in call:
+            rid, pid, _se = topo.addr(h)
+            mk = feed_mask(h, which)
+            trs.append(RemoteDMATransfer(dst_ids=[DstId(rid=rid, pnc=pid)], dma_engine_mask=mk,
+                                         remote_sem=S["arr%d" % me], src=slot(me), dst=slot(me)))
+            loc[0] += len(_bits(mk))
+        g.remote_dma_fused(trs, local_sem=S.loc)
     g.wait_ge(S.x, 16)
     put(bc, T.xs[:, :], S.xr, feed_mask(bc, "hi"))
     for e, q in plan["sends"][core]:
@@ -368,7 +379,6 @@ def rank_program(g, core, T, topo):
         P.wait_ge(S["pb%d" % h], len(_bits(topo.mask(bc, rc))))
         P.matmul(T["Y%d" % h][:, 0:HF], T.I[:, :], T.YB[:, h * HF:(h + 1) * HF], start=False,
                  stop=False).then_inc(S["l2_%d" % h], 1)
-    for h in (0, 1):
         P.wait_ge(S["rl_%d" % (LS + h)], 1)
         second(LAST, h)
 

from concourse.bass import DstId, RemoteDMATransfer
from concourse.mybir import AluOpType

NR = 8
TOK = 512
HF = TOK // 2
F = 128
WW = 2 * F
NB = 6
HEAD = 8
GROUP = (1, 2, 3)
CO = 2.0 ** 60

SCRATCH = {
    "Wall": ("sbuf", [128, NR * WW], "bfloat16"),
    "xs": ("sbuf", [128, TOK], "bfloat16"),
    "gs": ("sbuf", [128, TOK], "bfloat16"),
    "ones": ("sbuf", [128, F], "bfloat16"),
    "zeros": ("sbuf", [128, TOK], "bfloat16"),
    "gb": ("sbuf", [128, TOK], "bfloat16"),
    "R": ("sbuf", [128, TOK], "bfloat16"),
    "Cb": ("sbuf", [128, NR * F], "bfloat16"),
    "H": ("sbuf", [128, NR * TOK], "bfloat16"),
    "ysb": ("sbuf", [128, TOK], "bfloat16"),
    "YB": ("sbuf", [128, TOK], "bfloat16"),
    "D1": ("sbuf", [128, F + 1], "bfloat16"),
    "Dd": ("dram", [F + 1, 128], "bfloat16"),
    "I": ("sbuf", [128, F], "bfloat16"),
    "Y0": ("psum", [128, TOK], "float32"),
    "Y1": ("psum", [128, TOK], "float32"),
}
for _i in range(NB):
    SCRATCH["P%d" % _i] = ("psum", [128, TOK], "float32")

SEMAPHORES = ["w", "x", "g", "ms1", "msc", "msb", "msz", "gm", "gb", "r", "loc", "l2_0", "l2_1", "y0", "y1", "st0",
              "st1", "hms0", "hms1", "hsq0", "hsq1", "xr", "cbr", "pb0", "pb1", "id0", "id1", "id2"]
SEMAPHORES += ["arr%d" % _i for _i in range(NR)]
SEMAPHORES += ["l1_%d" % _i for _i in range(NR + 1)]
SEMAPHORES += ["rl_%d" % _i for _i in range(NR + 1)]


def _bits(mask):
    return [b for b in range(32) if (mask >> b) & 1]


def _mask(bitlist):
    m = 0
    for b in bitlist:
        m |= 1 << b
    return m


def _cover(route, a, b):
    out = []
    for v in sorted(set(route[a:b])):
        left = set(t for t in range(a, b) if route[t] == v)
        while left:
            pts = sorted(left)
            best = (pts[0], 1, 1)
            for i, s in enumerate(pts):
                for u in pts[i + 1:]:
                    d = u - s
                    n = 2
                    while s + n * d in left:
                        n += 1
                    if n > best[2]:
                        best = (s, d, n)
            for j in range(best[2]):
                left.remove(best[0] + j * best[1])
            out.append((v,) + best)
    return out


def _plan(T, topo):
    cores = list(T.cores)
    chips = [topo.chip(c) for c in cores]
    n = len(cores)
    every = range(topo.CORES_PER_CHIP * topo.CHIPS)
    first = sorted([r for r in range(n) if r == 0 or topo.same_plane(chips[r], chips[0])], key=lambda r: chips[r])
    second = [[q for q in range(n) if topo.mates(chips[q], chips[r])][0] for r in first]
    planes = [first, second]
    hop = 1.5
    sends, feeds, est = {}, {}, {}
    for pl in (0, 1):
        mine, other = planes[pl], planes[1 - pl]
        m = len(mine)
        for p, r in enumerate(mine):
            c = cores[r]
            same = [mine[(p + k) % m] for k in range(1, m)]
            cross = [other[(p + k) % m] for k in range(m)]
            near = [h for h in every if topo.chip(h) == chips[r] and h != c and topo.die(h) == topo.die(c)]
            owners = [h for h in near if topo.may_write(h, cores[cross[0]])]
            plain = [h for h in near if h not in owners]
            if topo.may_write(c, cores[cross[0]]):
                a, b = owners[0], plain[0]
                feeds[r] = [[(a, "lo"), (b, "hi")]]
                jobs = {c: [(same[0], 2.0), (cross[0], 3.0), (cross[1], 4.2)],
                        a: [(cross[2], 2.2 + hop), (cross[3], 3.2 + hop)],
                        b: [(same[1], 2.0 + hop), (same[2], 3.0 + hop)]}
            else:
                a, b = owners[0], owners[1]
                feeds[r] = [[(a, "lo"), (b, "hi")]]
                jobs = {c: [(same[0], 2.0), (same[1], 3.0), (same[2], 4.0)],
                        a: [(cross[0], 2.0 + hop), (cross[1], 3.2 + hop)],
                        b: [(cross[2], 2.2 + hop), (cross[3], 3.2 + hop)]}
            for s in jobs:
                sends[s] = [(r, q) for q, _t in jobs[s]]
                for q, t in jobs[s]:
                    est[(r, q)] = t
    order, bcore, land = {}, {}, {}
    for q in range(n):
        order[q] = [q] + sorted([e for e in range(n) if e != q], key=lambda e: (est[(e, q)], e))
        free = [h for h in every if topo.chip(h) == chips[q] and h != cores[q] and h not in sends]
        free.sort(key=lambda h: (topo.die(h) != topo.die(cores[q]), h))
        bcore[q] = free[0]
        for i, e in enumerate(order[q]):
            land[(e, q)] = bcore[q] if i in GROUP else cores[q]
    return {"sends": sends, "feeds": feeds, "order": order, "bcore": bcore, "land": land}


def rank_program(g, core, T, topo):
    cores = list(T.cores)
    S = T.sem
    chip = topo.chip(core)
    home = [r for r in range(len(cores)) if topo.chip(cores[r]) == chip]
    if not home:
        return
    r0 = home[0]
    rc = cores[r0]
    plan = _plan(T, topo)
    bc = plan["bcore"][r0]
    helpers = [h for h in range(topo.CORES_PER_CHIP * topo.CHIPS) if topo.chip(h) == chip and h != rc]
    far = [c for c in cores if topo.chip(c) != chip][0]
    route = [e[0] for e in T.tables["ROUTE"][r0]]
    seq_b = [plan["order"][r0][i] for i in GROUP]
    seq = [e for i, e in enumerate(plan["order"][r0]) if i not in GROUP]
    nblk = TOK // 8
    bounds = [0]
    for k in range(len(helpers)):
        bounds.append(bounds[-1] + 8 * (nblk // len(helpers) + (1 if k < nblk % len(helpers) else 0)))
    loc = [0]
    V = g.vector
    P = g.tensor
    LS = NR - 1

    def slot(e):
        return T.Wall[:, e * WW:(e + 1) * WW]

    def put(dst, ap, sem, mask, out=None):
        rid, pid, _se = topo.addr(dst)
        g.remote_dma(out_ap=(ap if out is None else out), in_ap=ap, remote_sem=sem, local_sem=S.loc, pid=pid,
                     routing_id=rid, dma_engine_mask=mask)
        loc[0] += len(_bits(mask))

    def code_lanes(h):
        on = topo.mask(h, rc)
        if h in plan["sends"]:
            return on & topo.mask(h, far)
        if h == bc:
            return on
        return _mask(_bits(on)[:4])

    def feed_mask(dst, which):
        on, off = topo.mask(rc, dst), topo.mask(rc, far)
        return (on & off) if which == "lo" else (on & ~off)

    def ship(e, q):
        dst = plan["land"][(e, q)]
        put(dst, slot(e), S["arr%d" % e], topo.mask(core, dst))

    def w1(e):
        return T.Wall[:, e * WW:e * WW + F]

    def w2(e):
        return T.Wall[:, e * WW + F:(e + 1) * WW]

    def coeffs(experts, base, sem):
        n = len(experts)
        V.memset(T.Cb[0:32, base * F:(base + n) * F], -CO).then_inc(sem, 1)
        for j, e in enumerate(experts):
            V.memset(T.Cb[32:64, (base + j) * F:(base + j + 1) * F], 2.0 * e * CO).then_inc(sem, 1)
            V.memset(T.Cb[64:128, (base + j) * F:(base + j + 1) * F], -0.5 * e * e * CO).then_inc(sem, 1)
        return 1 + 2 * n

    def n_arr(e):
        return len(_bits(topo.mask(cores[e], core)))

    if core != rc:
        k = helpers.index(core)
        a, b = bounds[k], bounds[k + 1]
        pieces = [(a, a + HEAD), (a + HEAD, b)]
        counts = []
        for i, (pa, pb) in enumerate(pieces):
            nms = 1
            V.memset(T.R[64:128, pa:pb], 1.0).then_inc(S["hms%d" % i], 1)
            for v, start, step, cnt in _cover(route, pa, pb):
                if cnt == 1 or step == 1:
                    ap = T.R[0:64, start:start + cnt]
                else:
                    ap = T.R[0:64, start:start + (cnt - 1) * step + 1:step]
                V.memset(ap, float(v)).then_inc(S["hms%d" % i], 1)
                nms += 1
            counts.append(nms)
            V.wait_ge(S["hms%d" % i], nms)
            V.tensor_tensor(T.R[0:32, pa:pb], T.R[0:32, pa:pb], T.R[0:32, pa:pb],
                            AluOpType.mult).then_inc(S["hsq%d" % i], 1)
            g.wait_ge(S["hms%d" % i], nms)
            g.wait_ge(S["hsq%d" % i], 1)
            put(rc, T.R[:, pa:pb], S.r, code_lanes(core))
            if core != bc:
                put(bc, T.R[:, pa:pb], S.r, code_lanes(core))
        jobs = plan["sends"].get(core, [])
        if jobs:
            which = [w for call in plan["feeds"][r0] for h, w in call if h == core][0]
            g.wait_ge(S["arr%d" % r0], len(_bits(feed_mask(core, which))))
            for e, q in jobs:
                ship(e, q)
        if core == bc:
            n = len(seq_b)
            LQ = n - 1
            V.memset(T.zeros[:, :], 0.0).then_inc(S.msz, 1)
            nown = coeffs(seq_b[1:], 1, S.msc)
            V.wait_ge(S.msz, 1)
            for j in range(LQ):
                V.wait_ge(S["l1_%d" % j], 1)
                V.tensor_tensor(T.H[:, j * TOK:(j + 1) * TOK], T["P%d" % j][:, :], T.zeros[:, :],
                                AluOpType.max).then_inc(S["rl_%d" % j], 1)
            for h in (0, 1):
                V.wait_ge(S["l1_%d" % (LS + h)], 1)
                V.tensor_tensor(T.H[:, LQ * TOK + h * HF:LQ * TOK + (h + 1) * HF], T["P%d" % (LQ + h)][:, 0:HF],
                                T.zeros[:, 0:HF], AluOpType.max).then_inc(S["rl_%d" % (LS + h)], 1)
            for h in (0, 1):
                V.wait_ge(S["l2_%d" % h], n)
                V.tensor_copy(T.ysb[:, h * HF:(h + 1) * HF], T["Y%d" % h][:, 0:HF]).then_inc(S["y%d" % h], 1)

            def sec(j, h):
                P.matmul(T["Y%d" % h][:, 0:HF], w2(seq_b[j]), T.H[:, j * TOK + h * HF:j * TOK + (h + 1) * HF],
                         start=(j == 0), stop=(j == n - 1)).then_inc(S["l2_%d" % h], 1)

            P.wait_ge(S.cbr, len(_bits(topo.mask(rc, bc))))
            P.wait_ge(S.msc, nown)
            for i in (0, 1):
                P.wait_ge(S["hms%d" % i], counts[i])
                P.wait_ge(S["hsq%d" % i], 1)
            P.wait_ge(S.r, 2 * sum(len(_bits(code_lanes(h))) for h in helpers if h != bc))
            for j in range(LQ):
                P.matmul(T["P%d" % j][:, :], T.Cb[:, j * F:(j + 1) * F], T.R[:, :], start=True, stop=False)
            for h in (0, 1):
                P.matmul(T["P%d" % (LQ + h)][:, 0:HF], T.Cb[:, LQ * F:(LQ + 1) * F], T.R[:, h * HF:(h + 1) * HF],
                         start=True, stop=False)
            P.wait_ge(S.xr, len(_bits(feed_mask(bc, "hi"))))
            for j in range(n):
                P.wait_ge(S["arr%d" % seq_b[j]], n_arr(seq_b[j]))
                if j < LQ:
                    P.matmul(T["P%d" % j][:, :], w1(seq_b[j]), T.xs[:, :], start=False,
                             stop=True).then_inc(S["l1_%d" % j], 1)
                else:
                    for h in (0, 1):
                        P.matmul(T["P%d" % (LQ + h)][:, 0:HF], w1(seq_b[j]), T.xs[:, h * HF:(h + 1) * HF],
                                 start=False, stop=True).then_inc(S["l1_%d" % (LS + h)], 1)
                if j >= 1:
                    P.wait_ge(S["rl_%d" % (j - 1)], 1)
                    sec(j - 1, 0)
                    sec(j - 1, 1)
            for h in (0, 1):
                P.wait_ge(S["rl_%d" % (LS + h)], 1)
                sec(LQ, h)
            for h in (0, 1):
                g.wait_ge(S["y%d" % h], 1)
                put(rc, T.ysb[:, h * HF:(h + 1) * HF], S["pb%d" % h], topo.mask(core, rc),
                    out=T.YB[:, h * HF:(h + 1) * HF])
        g.wait_ge(S.loc, loc[0])
        return

    me = r0
    n = len(seq)
    LAST = n - 1
    LB = [LAST % NB, (LAST + 1) % NB]

    g.sync.dma_start(T.Wall[:, me * WW:me * WW + F], T.w1[:, :]).then_inc(S.w, 16)
    g.scalar.dma_start(T.Wall[:, me * WW + F:(me + 1) * WW], T.w2[:, :]).then_inc(S.w, 16)
    g.sync.dma_start(T.xs[:, :], T.x[:, :]).then_inc(S.x, 16)
    g.scalar.dma_start(T.gs[0:1, :], T.gate[:, :]).then_inc(S.g, 16)
    g.sync.wait_ge(S.id0, 2)
    g.sync.dma_start(T.Dd[:, :], T.D1[:, :]).then_inc(S.id1, 16)
    g.sync.wait_ge(S.id1, 16)
    g.sync.dma_start(T.I[:, :], T.Dd[0:128, :]).then_inc(S.id2, 16)

    ncb = coeffs(seq_b[:1], n, S.msb)
    V.memset(T.ones[0:1, :], 1.0).then_inc(S.ms1, 1)
    nc = coeffs(seq, 0, S.msc)
    V.memset(T.zeros[:, :], 0.0).then_inc(S.msz, 1)
    V.memset(T.D1[:, 0:1], 1.0).then_inc(S.id0, 1)
    V.memset(T.D1[:, 1:F + 1], 0.0).then_inc(S.id0, 1)

    g.wait_ge(S.msb, ncb)
    put(bc, T.Cb[:, n * F:(n + 1) * F], S.cbr, topo.mask(rc, bc), out=T.Cb[:, 0:F])
    g.wait_ge(S.w, 32)
    for call in plan["feeds"][me]:
        trs = []
        for h, which in call:
            rid, pid, _se = topo.addr(h)
            mk = feed_mask(h, which)
            trs.append(RemoteDMATransfer(dst_ids=[DstId(rid=rid, pnc=pid)], dma_engine_mask=mk,
                                         remote_sem=S["arr%d" % me], src=slot(me), dst=slot(me)))
            loc[0] += len(_bits(mk))
        g.remote_dma_fused(trs, local_sem=S.loc)
    g.wait_ge(S.x, 16)
    put(bc, T.xs[:, :], S.xr, feed_mask(bc, "hi"))
    for e, q in plan["sends"][core]:
        ship(e, q)
    g.wait_ge(S.loc, loc[0])

    V.wait_ge(S.gm, 1)
    V.tensor_copy(T.gb[:, :], T.Y0[:, :]).then_inc(S.gb, 1)
    V.wait_ge(S.msz, 1)
    for j in range(LAST):
        V.wait_ge(S["l1_%d" % j], 1)
        V.tensor_tensor(T.H[:, j * TOK:(j + 1) * TOK], T["P%d" % j][:, :], T.zeros[:, :],
                        AluOpType.max).then_inc(S["rl_%d" % j], 1)
    for h in (0, 1):
        V.wait_ge(S["l1_%d" % (LS + h)], 1)
        V.tensor_tensor(T.H[:, LAST * TOK + h * HF:LAST * TOK + (h + 1) * HF], T["P%d" % LB[h]][:, 0:HF],
                        T.zeros[:, 0:HF], AluOpType.max).then_inc(S["rl_%d" % (LS + h)], 1)
    V.wait_ge(S.gb, 1)
    for h in (0, 1):
        V.wait_ge(S["l2_%d" % h], n + 1)
        V.tensor_tensor(T.ysb[:, h * HF:(h + 1) * HF], T["Y%d" % h][:, 0:HF], T.gb[:, h * HF:(h + 1) * HF],
                        AluOpType.mult).then_inc(S["y%d" % h], 1)

    n_r = 2 * sum(len(_bits(code_lanes(h))) for h in helpers)

    def cb(j):
        return T.Cb[:, j * F:(j + 1) * F]

    def second(j, h):
        P.matmul(T["Y%d" % h][:, 0:HF], w2(seq[j]), T.H[:, j * TOK + h * HF:j * TOK + (h + 1) * HF], start=(j == 0),
                 stop=(j == LAST)).then_inc(S["l2_%d" % h], 1)

    def last_bias(h):
        P.matmul(T["P%d" % LB[h]][:, 0:HF], cb(LAST), T.R[:, h * HF:(h + 1) * HF], start=True, stop=False)

    P.wait_ge(S.ms1, 1)
    P.wait_ge(S.g, 16)
    P.matmul(T.Y0[:, :], T.ones[0:1, :], T.gs[0:1, :], start=True, stop=True).then_inc(S.gm, 1)
    P.wait_ge(S.w, 32)
    P.wait_ge(S.x, 16)
    P.matmul(T.P0[:, :], w1(me), T.xs[:, :], start=True, stop=False)
    P.wait_ge(S.msc, nc)
    P.wait_ge(S.r, n_r)
    P.matmul(T.P0[:, :], cb(0), T.R[:, :], start=False, stop=True).then_inc(S.l1_0, 1)
    for j in range(1, LAST):
        P.matmul(T["P%d" % j][:, :], cb(j), T.R[:, :], start=True, stop=False)
    for h in (0, 1):
        if LB[h] != 0:
            last_bias(h)
    P.wait_ge(S.gb, 1)
    P.wait_ge(S.rl_0, 1)
    second(0, 0)
    second(0, 1)
    for h in (0, 1):
        if LB[h] == 0:
            last_bias(h)
    for j in range(1, n):
        e = seq[j]
        P.wait_ge(S["arr%d" % e], n_arr(e))
        if j < LAST:
            P.matmul(T["P%d" % j][:, :], w1(e), T.xs[:, :], start=False, stop=True).then_inc(S["l1_%d" % j], 1)
        else:
            for h in (0, 1):
                P.matmul(T["P%d" % LB[h]][:, 0:HF], w1(e), T.xs[:, h * HF:(h + 1) * HF], start=False,
                         stop=True).then_inc(S["l1_%d" % (LS + h)], 1)
        if j >= 2:
            P.wait_ge(S["rl_%d" % (j - 1)], 1)
            second(j - 1, 0)
            second(j - 1, 1)
    P.wait_ge(S.id2, 16)
    for h in (0, 1):
        P.wait_ge(S["pb%d" % h], len(_bits(topo.mask(bc, rc))))
        P.matmul(T["Y%d" % h][:, 0:HF], T.I[:, :], T.YB[:, h * HF:(h + 1) * HF], start=False,
                 stop=False).then_inc(S["l2_%d" % h], 1)
        P.wait_ge(S["rl_%d" % (LS + h)], 1)
        second(LAST, h)

    g.sync.wait_ge(S.y0, 1)
    g.sync.dma_start(T.y[:, 0:HF], T.ysb[:, 0:HF]).then_inc(S.st0, 16)
    g.sync.wait_ge(S.st0, 16)
    g.scalar.wait_ge(S.y1, 1)
    g.scalar.dma_start(T.y[:, HF:TOK], T.ysb[:, HF:TOK]).then_inc(S.st1, 16)
    g.scalar.wait_ge(S.st1, 16)
